import numpy as np
import ml_dtypes


def mxq(x, axis, fmt="e4m3"):
    dtype, down = {"e4m3": (ml_dtypes.float8_e4m3fn, 7), "e5m2": (ml_dtypes.float8_e5m2, 14)}[fmt]
    v = np.moveaxis(np.asarray(x, np.float32).astype(ml_dtypes.bfloat16).astype(np.float64), axis, -1)
    blocks = v.reshape(v.shape[:-1] + (-1, 32))
    amax = np.abs(blocks).max(-1, keepdims=True)
    byte = np.maximum(np.where(amax > 0, np.frexp(amax)[1] - 1 + 127, 0) - down, 1)
    scale = np.exp2(byte - 127.0)
    codes = (blocks / scale).astype(np.float32).astype(dtype).astype(np.float64)
    return np.moveaxis((codes * scale).reshape(v.shape), -1, axis)


WIDE = False


def mx_kscale(k):
    if not WIDE:
        return np.ones(k)
    levels = np.array([10, -10, 5, -5, 0])
    if k % 512:
        return np.exp2(np.random.permutation(np.resize(levels, k // 32))).repeat(32)
    a = np.empty((k // 512, 16))
    for p in range(k // 512):
        a[p, :8] = np.random.permutation(np.resize(levels, 8))
        for g in range(8):
            far = levels[np.abs(levels - a[p, g]) >= 10]
            a[p, g + 8] = far[np.random.randint(len(far))]
    return np.exp2(a.ravel()).repeat(32)


def f64(x):
    return np.asarray(x).astype(np.float64)


def striped(idx):
    return np.tile(idx.reshape(-1, 16).T, (8, 1)).astype(np.uint16)


def unstriped(offs):
    return offs[:16].T.reshape(-1).astype(np.int64)


E2M1 = np.array([0.0, 0.5, 1.0, 1.5, 2.0, 3.0, 4.0, 6.0, -0.0, -0.5, -1.0, -1.5, -2.0, -3.0, -4.0, -6.0])


def pack_weight(w, fmt):
    k, n = w.shape
    w = f64(np.asarray(w, np.float32).astype(ml_dtypes.bfloat16)).reshape(k // 32, 32, n)
    amax = np.abs(w).max(1)
    if fmt == "e4m3":
        byte = np.frexp(amax)[1] - 1 + 127 - 7
    else:
        mant, ex = np.frexp(amax / 6.0)
        byte = np.where(mant > 0.5, ex, ex - 1) + 127
    byte = np.clip(np.where(amax > 0, byte, 1), 1, 254)
    scaled = (w * np.exp2(127.0 - byte)[:, None, :]).reshape(k, n).astype(np.float32)
    by_word = np.ascontiguousarray(scaled.reshape(k // 512, 128, 4, n).transpose(0, 1, 3, 2))
    if fmt == "e4m3":
        words = by_word.astype(ml_dtypes.float8_e4m3fn).view(np.uint8)
    else:
        c = by_word.astype(ml_dtypes.float4_e2m1fn).view(np.uint8) & 0xF
        words = (c[..., 0::2] | (c[..., 1::2] << 4)).reshape(k // 512, 128, 2 * n)
    return np.ascontiguousarray(words), np.ascontiguousarray(byte.astype(np.uint8).reshape(k // 512, 16, n))


def unpack_weight(words, scales, fmt):
    g, _, n = scales.shape
    words = np.ascontiguousarray(words).reshape(g, 128, n, -1)
    if fmt == "e4m3":
        vals = words.view(ml_dtypes.float8_e4m3fn).astype(np.float64)
    else:
        nib = np.empty((g, 128, n, 4), np.uint8)
        nib[..., 0::2] = words & 0xF
        nib[..., 1::2] = words >> 4
        vals = E2M1[nib]
    vals = vals * np.repeat(np.exp2(scales.astype(np.float64) - 127.0), 8, axis=1)[..., None]
    return vals.transpose(0, 1, 3, 2).reshape(g * 512, n)


def gelu(v):
    return 0.5 * v * (1.0 + np.tanh(np.sqrt(2.0 / np.pi) * (v + 0.044715 * v**3)))


def striped8(idx):
    return np.concatenate([v.reshape(-1, 16).T for v in idx]).astype(np.uint16)


def unstriped8(offs):
    return np.stack([offs[16 * g:16 * g + 16].T.reshape(-1) for g in range(8)]).astype(np.int64)


def heads(h, wgt, idx8):
    r = np.arange(h.shape[0])
    return wgt[r // 4 % 128] * h[r[:, None], idx8[r % 512 // 64]]


def bf(x):
    return np.asarray(x, np.float32).astype(ml_dtypes.bfloat16)


def planes(Y):
    n, m = Y.shape
    b = f64(bf(Y)).reshape(n // 32, 32, m)
    amax = np.abs(b).max(1)
    byte = np.clip(np.where(amax > 0, np.frexp(amax)[1] - 1 + 127 - 7, 1), 1, 254)
    codes = (b * np.exp2(127.0 - byte)[:, None, :]).reshape(n, m).astype(np.float32).astype(ml_dtypes.float8_e4m3fn).view(np.uint8)
    words = codes.reshape(n // 512, 128, 4, m).transpose(0, 1, 3, 2)
    return np.ascontiguousarray(words), np.ascontiguousarray(byte.astype(np.uint8).reshape(n // 512, 16, m))


K, H, N, T, S, P = 512, 1024, 1024, 4096, 1024, 512

def setup_inputs():
    n = np.random.standard_normal
    s = mx_kscale(K)[:, None]
    u = mx_kscale(H)[:, None]
    size = np.exp(0.8 * n(N))
    tab_words, tab_scales = pack_weight(n((K, T)) * s, "e4m3")
    w2_words, w2_scales = pack_weight(n((K, H)) / np.sqrt(K) / s * u.T, "e2m1")
    w4_words, w4_scales = pack_weight(n((H, N)) / np.sqrt(H) / u * size, "e2m1")
    return {
        "tab_words": tab_words, "tab_scales": tab_scales,
        "offs": striped(np.random.permutation(T)[:S]),
        "w1": (n((K, H)) / np.sqrt(K) / s * u.T).astype(np.float32),
        "b1": (0.5 * n(H) * u[:, 0]).astype(np.float32),
        "w2_words": w2_words, "w2_scales": w2_scales,
        "w3": (n((K, H)) / np.sqrt(K) / s).astype(np.float32),
        "b3": (0.7 * n(H)).astype(np.float32),
        "offs2": striped8(np.stack([np.random.permutation(S)[:P] for _ in range(8)])),
        "offs3": striped8(np.stack([np.random.permutation(S)[:P] for _ in range(8)])),
        "wga": np.repeat(np.random.uniform(0.5, 2.0, (8, P)), 16, axis=0).astype(np.float32),
        "wgb": np.repeat(np.random.uniform(0.5, 2.0, (8, P)), 16, axis=0).astype(np.float32),
        "w4_words": w4_words, "w4_scales": w4_scales,
        "sed": (0.8 * n((N, P)) * size[:, None]).astype(np.float32),
    }

def reference(tab_words, tab_scales, offs, w1, b1, w2_words, w2_scales, w3, b3, offs2, offs3, wga, wgb, w4_words, w4_scales, sed):
    v = unpack_weight(tab_words, tab_scales, "e4m3")[:, unstriped(offs)]
    w2 = unpack_weight(w2_words, w2_scales, "e2m1")
    w4 = unpack_weight(w4_words, w4_scales, "e2m1")
    d1 = (mxq(f64(w1), 0, "e4m3").T @ v) + f64(b1)[:, None]
    h1 = np.maximum(d1, w2.T @ v)
    h2 = (mxq(f64(w3), 0, "e4m3").T @ v) + f64(b3)[:, None]
    xa = heads(h1, f64(wga), unstriped8(offs2))
    xb = heads(h2, f64(wgb), unstriped8(offs3))
    z = xa * np.tanh(xb)
    y = (w4.T @ mxq(z, 0, "e4m3")) + f64(sed)
    words, scales = planes(y)
    return y, words, scales

@@ -1,0 +1,296 @@
+from contextlib import ExitStack
+
+import concourse.mybir as mybir
+
+K, H, N, T, S, M = 512, 1024, 1024, 4096, 1024, 512
+FLOPS = 2 * (3 * K * H * S + H * N * M)
+
+F32 = mybir.dt.float32
+BF16 = mybir.dt.bfloat16
+I32 = mybir.dt.int32
+U32 = mybir.dt.uint32
+U16 = mybir.dt.uint16
+U8 = mybir.dt.uint8
+FP8X4 = mybir.dt.float8_e4m3fn_x4
+FP4X4 = mybir.dt.float4_e2m1fn_x4
+ACT = mybir.ActivationFunctionType
+ALU = mybir.AluOpType
+P = 128
+BANK = 512
+
+
+def tile_list_seagrass_clone_mixing_kernel(
+    tc, tab_words, tab_scales, offs, w1, b1, w2_words, w2_scales, w3, b3, offs2, offs3,
+    wga, wgb, w4_words, w4_scales, sed, out_0, out_1, out_2,
+):
+    nc = tc.nc
+    with ExitStack() as ctx:
+        held = ctx.enter_context(tc.tile_pool(name="held", bufs=1))
+        ring = ctx.enter_context(tc.tile_pool(name="ring", bufs=2))
+        psum = ctx.enter_context(tc.psum_pool(name="psum", bufs=8))
+
+        def keep(name, shape, dtype):
+            return held.tile(shape, dtype, name=name, align_bytes=64)
+
+        list1 = held.tile([P, S // 16], U16, name="list1")
+        list2 = held.tile([P, M // 16], U16, name="list2")
+        list3 = held.tile([P, M // 16], U16, name="list3")
+        tabs = held.tile([P, T], U8, name="tabs", tag="bytes", align_bytes=64)
+        packed = held.tile([P, H], U8, name="packed", tag="packed", align_bytes=64)
+        packed4 = keep("packed4", [P, N], U8)
+        dealt4 = keep("dealt4", [P, N], U8)
+        w2raw = held.tile([P, 2 * H], U8, name="w2raw", tag="big", align_bytes=64)
+        w2c = keep("w2c", [P, 2 * H], U8)
+        w4c = [keep(f"w4c{a}", [P, 2 * N], U8) for a in range(2)]
+        wraw = {}
+        wc = {(n, b): held.tile([P, BANK], U32, name=f"wc{n}{b}", tag=f"wc{n}{b}", align_bytes=64) for n in (1, 3) for b in range(2)}
+        ws = {(n, b): keep(f"ws{n}{b}", [P, BANK], U8) for n in (1, 3) for b in range(2)}
+        bias1 = keep("bias1", [P, 8], F32)
+        bias3 = keep("bias3", [P, 8], F32)
+        vc = [keep(f"vc{h}", [P, BANK], U32) for h in range(2)]
+        vs = keep("vs", [P, S], U8)
+        zc = [keep(f"zc{b}", [P, M], U32) for b in range(2)]
+        zs = [keep(f"zs{b}", [P, M], U8) for b in range(2)]
+        yc = [keep(f"yc{g}", [P, M], U32) for g in range(2)]
+        ys = [keep(f"ys{g}", [P, M], U8) for g in range(2)]
+        xa = [held.tile([P, 4, M], F32, name=f"xa{b}", tag=f"xa{b}", align_bytes=64) for b in range(2)]
+        th = [keep(f"th{b}", [P, 4, M], F32) for b in range(2)]
+        y = [keep(f"y{g}", [P, 4, M], F32) for g in range(2)]
+
+        def load_w(n, src, b, dst):
+            wraw[n, b] = dst
+            nc.sync.dma_start(out=dst, in_=src[:, BANK * b : BANK * (b + 1)].rearrange("(p j) c -> p j c", j=4))
+
+        def stage(name):
+            return held.tile([P, 4, BANK], F32, name=name, tag="stage", align_bytes=64)
+
+        nc.vector.memset(tabs[:].bitcast(I32), 0)
+        nc.gpsimd.memset(packed[:].bitcast(I32), 0)
+        for q in range(4):
+            nc.gpsimd.dma_start(
+                out=packed[32 * q : 32 * q + 4, :].bitcast(I32),
+                in_=w2_scales[0, 4 * q : 4 * q + 4, :].bitcast(I32),
+            )
+        nc.gpsimd.memset(packed4[:].bitcast(I32), 0)
+        for q in range(4):
+            nc.gpsimd.dma_start(
+                out=packed4[32 * q + 4 : 32 * q + 12, :].bitcast(I32),
+                in_=w4_scales[:, 4 * q : 4 * q + 4, :].bitcast(I32),
+            )
+        nc.gpsimd.tensor_copy(
+            out=dealt4[:].rearrange("p (b i q) -> p b i q", b=2, i=4),
+            in_=packed4[:].rearrange("p (b q i) -> p b i q", b=2, i=4),
+        )
+
+        nc.sync.dma_start(out=w2raw[:].bitcast(I32), in_=w2_words[0].bitcast(I32))
+        nc.sync.dma_start(out=list1[:], in_=offs)
+        nc.sync.dma_start(
+            out=bias1[:].rearrange("p (b i) -> p b i", b=2),
+            in_=b1.rearrange("(b p i) -> p b i", b=2, i=4),
+        )
+        nc.sync.dma_start(out=list2[:], in_=offs2)
+        load_w(1, w1, 0, stage("w10")[:])
+        nc.sync.dma_start(out=list3[:], in_=offs3)
+        nc.sync.dma_start(
+            out=bias3[:].rearrange("p (b i) -> p b i", b=2),
+            in_=b3.rearrange("(b p i) -> p b i", b=2, i=4),
+        )
+        for q in range(4):
+            nc.scalar.dma_start(
+                out=tabs[32 * q : 32 * q + 4, :].bitcast(I32),
+                in_=tab_scales[0, 4 * q : 4 * q + 4, :].bitcast(I32),
+            )
+
+        def load_sed(g, dst):
+            nc.sync.dma_start(
+                out=dst[:], in_=sed[BANK * g : BANK * (g + 1), :].rearrange("(p t) m -> p t m", t=4)
+            )
+            return dst
+
+        def round_w(n, b):
+            if (n, b) == (1, 0):
+                wb = held.tile([P, 4, P, 4], BF16, name="wb_first", tag="first", align_bytes=64)
+            else:
+                wb = ring.tile([P, 4, P, 4], BF16, name="wb", align_bytes=64)
+            nc.scalar.copy(
+                out=wb[:].rearrange("p i q j -> p q j i"),
+                in_=wraw[n, b].rearrange("p j (q i) -> p q j i", i=4),
+            )
+            return wb
+
+        def quant_w(n, b, wb):
+            nc.vector.quantize_mx(
+                out=wc[n, b][:].bitcast(FP8X4),
+                scales=ws[n, b][:],
+                in_=wb[:].rearrange("p i q j -> p (i q j)"),
+            )
+
+        def deal_words(copy, dst, src):
+            copy(
+                out=dst.bitcast(U16).rearrange("p (b i c q) -> p b c i q", b=2, i=4, q=8),
+                in_=src.bitcast(U16).rearrange("p (b c q i) -> p b c i q", b=2, i=4, q=8),
+            )
+
+        deal_words(nc.vector.tensor_copy, w2c[:], w2raw[:])
+        tabw = held.tile([P, T], U32, name="tabw", tag="big", align_bytes=64)
+        nc.sync.dma_start(
+            out=tabw[:].bitcast(I32),
+            in_=tab_words[0].rearrange("p t i -> p (t i)").bitcast(I32),
+        )
+        wb10 = round_w(1, 0)
+        nc.vector.tensor_copy(out=vs[:], in_=tabs[:].indirect(list1[:]))
+        load_w(3, w3, 0, stage("w30")[:])
+        quant_w(1, 0, wb10)
+        dealt = held.tile([P, H], U8, name="dealt", tag="first", align_bytes=64)
+        nc.vector.tensor_copy(
+            out=dealt[:].rearrange("p (b i q) -> p b i q", b=2, i=4),
+            in_=packed[:].rearrange("p (b q i) -> p b i q", b=2, i=4),
+        )
+        gab = held.tile([P, 2, M], F32, name="gab", tag="packed", align_bytes=64)
+        ga, gb = gab[:, 0, :], gab[:, 1, :]
+        nc.sync.dma_start(out=ga, in_=wga)
+        nc.sync.dma_start(out=gb, in_=wgb)
+        for h in range(2):
+            nc.vector.tensor_copy(out=vc[h][:], in_=tabw[:].indirect(list1[:, 32 * h : 32 * (h + 1)]))
+        late = held.tile([P, 2, 4, BANK], F32, name="late", tag="big", align_bytes=64)
+        load_w(1, w1, 1, late[:, 0])
+        load_w(3, w3, 1, late[:, 1])
+
+        def product8(n, s, h):
+            b, i = divmod(s, 4)
+            acc = psum.tile([P, BANK], F32, name="acc")
+            nc.tensor.matmul_mx(
+                out=acc[:],
+                lhsT=wc[n, b][:, P * i : P * (i + 1)].bitcast(FP8X4),
+                lhsT_scale=ws[n, b][:, P * i : P * (i + 1)],
+                rhs=vc[h][:].bitcast(FP8X4),
+                rhs_scale=vs[:, BANK * h : BANK * (h + 1)],
+                start=True, stop=True,
+            )
+            return acc
+
+        def product4(s, h):
+            acc = psum.tile([P, BANK], F32, name="acc")
+            nc.tensor.matmul_mx(
+                out=acc[:],
+                lhsT=w2c[:, 2 * P * s : 2 * P * (s + 1)].bitcast(FP4X4),
+                lhsT_scale=dealt[:, P * s : P * (s + 1)],
+                rhs=vc[h][:].bitcast(FP8X4),
+                rhs_scale=vs[:, BANK * h : BANK * (h + 1)],
+                start=True, stop=True,
+            )
+            return acc
+
+        def donor(s):
+            b, i = divmod(s, 4)
+            h1 = ring.tile([P, S], F32, name="h1")
+            for h in range(2):
+                cols = slice(BANK * h, BANK * (h + 1))
+                first = product8(1, s, h)
+                second = product4(s, h)
+                d1 = ring.tile([P, BANK], F32, name="d1", bufs=4)
+                nc.scalar.activation(out=d1[:], in_=first[:], func=ACT.Identity, bias=bias1[:, s : s + 1])
+                nc.vector.tensor_tensor(out=h1[:, cols], in0=second[:], in1=d1[:], op=ALU.max)
+            nc.vector.tensor_tensor(out=xa[b][:, i, :], in0=h1[:].indirect(list2[:]), in1=ga, op=ALU.mult)
+
+        def recipient(s):
+            b, i = divmod(s, 4)
+            h2 = ring.tile([P, S], F32, name="h2", bufs=3)
+            for h in range(2):
+                third = product8(3, s, h)
+                nc.scalar.activation(
+                    out=h2[:, BANK * h : BANK * (h + 1)], in_=third[:], func=ACT.Identity, bias=bias3[:, s : s + 1]
+                )
+            xb = ring.tile([P, M], F32, name="xb")
+            nc.vector.tensor_tensor(out=xb[:], in0=h2[:].indirect(list3[:]), in1=gb, op=ALU.mult)
+            nc.scalar.activation(out=th[b][:, i, :], in_=xb[:], func=ACT.Tanh)
+
+        def make_z(b):
+            zb = ring.tile([P, M, 4], BF16, name="zb", align_bytes=64)
+            nc.vector.tensor_tensor(
+                out=zb[:].rearrange("p (c e) i -> p c i e", e=4),
+                in0=xa[b][:].rearrange("p i (c e) -> p c i e", e=4),
+                in1=th[b][:].rearrange("p i (c e) -> p c i e", e=4),
+                op=ALU.mult,
+            )
+            return zb
+
+        def quant_z(b, zb):
+            nc.vector.quantize_mx(out=zc[b][:].bitcast(FP8X4), scales=zs[b][:], in_=zb[:].rearrange("p m i -> p (m i)"))
+
+        def last_pass(acc, s, a):
+            nc.tensor.matmul_mx(
+                out=acc[:],
+                lhsT=w4c[a][:, 2 * P * s : 2 * P * (s + 1)].bitcast(FP4X4),
+                lhsT_scale=w4s[:, a, P * s : P * (s + 1)],
+                rhs=zc[a][:].bitcast(FP8X4),
+                rhs_scale=zs[a][:],
+                start=(a == 0), stop=(a == 1),
+            )
+
+        donor(0)
+        donor(1)
+        quant_w(3, 0, round_w(3, 0))
+        sedt = [load_sed(0, stage("sed0"))]
+        donor(2)
+        recipient(0)
+        donor(3)
+        w4s = held.tile([P, 2, N], U8, name="w4s", tag="wc10", align_bytes=64)
+        nc.gpsimd.memset(w4s[:].rearrange("p a c -> p (a c)").bitcast(I32), 0)
+        for a in range(2):
+            for q in range(4):
+                nc.sync.dma_start(
+                    out=w4s[32 * q : 32 * q + 4, a, :].bitcast(I32),
+                    in_=dealt4[32 * q + 4 + 4 * a : 32 * q + 8 + 4 * a, :].bitcast(I32),
+                )
+        recipient(1)
+        quant_w(1, 1, round_w(1, 1))
+        recipient(2)
+        recipient(3)
+        donor(4)
+        wb31 = round_w(3, 1)
+        w4raw = held.tile([P, 2, 2 * N], U8, name="w4raw", tag="big", align_bytes=64)
+        for a in range(2):
+            nc.sync.dma_start(out=w4raw[:, a, :].bitcast(I32), in_=w4_words[a].bitcast(I32))
+        zb0 = make_z(0)
+        quant_w(3, 1, wb31)
+        sedt.append(load_sed(1, held.tile([P, 4, M], F32, name="sed1", tag="xa0", align_bytes=64)))
+        donor(5)
+        quant_z(0, zb0)
+        recipient(4)
+        donor(6)
+        recipient(5)
+        recipient(6)
+        recipient(7)
+        donor(7)
+        for a in range(2):
+            deal_words(nc.scalar.copy, w4c[a][:], w4raw[:, a, :])
+        accs = [psum.tile([P, BANK], F32, name="acc") for s in range(8)]
+        for s in range(8):
+            last_pass(accs[s], s, 0)
+        quant_z(1, make_z(1))
+        for s in range(8):
+            last_pass(accs[s], s, 1)
+        for g in range(2):
+            for t in range(4):
+                nc.vector.tensor_tensor(out=y[g][:, t, :], in0=accs[4 * g + t][:], in1=sedt[g][:, t, :], op=ALU.add)
+            nc.sync.dma_start(
+                out=out_0[BANK * g : BANK * (g + 1), :].rearrange("(p t) m -> p t m", t=4), in_=y[g][:]
+            )
+        for g in range(2):
+            yb = ring.tile([P, M, 4], BF16, name="yb", align_bytes=64)
+            src = y[g][:].rearrange("p t (c e) -> p c t e", e=4)
+            dst = yb[:].rearrange("p (c e) t -> p c t e", e=4)
+            if g == 0:
+                nc.scalar.copy(out=dst, in_=src)
+            else:
+                nc.vector.tensor_copy(out=dst, in_=src)
+            nc.vector.quantize_mx(out=yc[g][:].bitcast(FP8X4), scales=ys[g][:], in_=yb[:].rearrange("p m t -> p (m t)"))
+            nc.sync.dma_start(
+                out=out_1[g].rearrange("p m t -> p (m t)").bitcast(I32), in_=yc[g][:].bitcast(I32)
+            )
+            for q in range(4):
+                nc.scalar.dma_start(
+                    out=out_2[g, 4 * q : 4 * q + 4, :].bitcast(I32),
+                    in_=ys[g][32 * q : 32 * q + 4, :].bitcast(I32),
+                )

@@ -49,13 +49,12 @@ def tile_list_seagrass_clone_mixing_kernel(
         bias3 = keep("bias3", [P, 8], F32)
         vc = [keep(f"vc{h}", [P, BANK], U32) for h in range(2)]
         vs = keep("vs", [P, S], U8)
+        picked = keep("picked", [P, S], U8)
         zc = [keep(f"zc{b}", [P, M], U32) for b in range(2)]
         zs = [keep(f"zs{b}", [P, M], U8) for b in range(2)]
-        yc = [keep(f"yc{g}", [P, M], U32) for g in range(2)]
-        ys = [keep(f"ys{g}", [P, M], U8) for g in range(2)]
+        ys = keep("ys", [P, 2, M], U8)
         xa = [held.tile([P, 4, M], F32, name=f"xa{b}", tag=f"xa{b}", align_bytes=64) for b in range(2)]
         th = [keep(f"th{b}", [P, 4, M], F32) for b in range(2)]
-        y = [keep(f"y{g}", [P, 4, M], F32) for g in range(2)]
 
         def load_w(n, src, b, dst):
             wraw[n, b] = dst
@@ -71,6 +70,7 @@ def tile_list_seagrass_clone_mixing_kernel(
                 out=packed[32 * q : 32 * q + 4, :].bitcast(I32),
                 in_=w2_scales[0, 4 * q : 4 * q + 4, :].bitcast(I32),
             )
+        nc.gpsimd.memset(vs[:].bitcast(I32), 0)
         nc.gpsimd.memset(packed4[:].bitcast(I32), 0)
         for q in range(4):
             nc.gpsimd.dma_start(
@@ -95,11 +95,7 @@ def tile_list_seagrass_clone_mixing_kernel(
             out=bias3[:].rearrange("p (b i) -> p b i", b=2),
             in_=b3.rearrange("(b p i) -> p b i", b=2, i=4),
         )
-        for q in range(4):
-            nc.scalar.dma_start(
-                out=tabs[32 * q : 32 * q + 4, :].bitcast(I32),
-                in_=tab_scales[0, 4 * q : 4 * q + 4, :].bitcast(I32),
-            )
+        nc.scalar.dma_start(out=tabs[0:P:8, :].bitcast(I32), in_=tab_scales[0].bitcast(I32))
 
         def load_sed(g, dst):
             nc.sync.dma_start(
@@ -138,8 +134,13 @@ def tile_list_seagrass_clone_mixing_kernel(
             in_=tab_words[0].rearrange("p t i -> p (t i)").bitcast(I32),
         )
         wb10 = round_w(1, 0)
-        nc.vector.tensor_copy(out=vs[:], in_=tabs[:].indirect(list1[:]))
-        load_w(3, w3, 0, stage("w30")[:])
+        nc.vector.tensor_copy(out=picked[:], in_=tabs[:].indirect(list1[:]))
+        for q in range(4):
+            nc.sync.dma_start(
+                out=vs[32 * q : 32 * q + 4, :].bitcast(I32),
+                in_=picked[32 * q : 32 * q + 32 : 8, :].bitcast(I32),
+            )
+        load_w(1, w1, 1, stage("w11")[:])
         quant_w(1, 0, wb10)
         dealt = held.tile([P, H], U8, name="dealt", tag="first", align_bytes=64)
         nc.vector.tensor_copy(
@@ -153,7 +154,7 @@ def tile_list_seagrass_clone_mixing_kernel(
         for h in range(2):
             nc.vector.tensor_copy(out=vc[h][:], in_=tabw[:].indirect(list1[:, 32 * h : 32 * (h + 1)]))
         late = held.tile([P, 2, 4, BANK], F32, name="late", tag="big", align_bytes=64)
-        load_w(1, w1, 1, late[:, 0])
+        load_w(3, w3, 0, late[:, 0])
         load_w(3, w3, 1, late[:, 1])
 
         def product8(n, s, h):
@@ -181,59 +182,106 @@ def tile_list_seagrass_clone_mixing_kernel(
             )
             return acc
 
+        h1, h2 = {}, {}
+        whole = slice(0, M)
+        halves = [slice(0, M // 2), slice(M // 2, M)]
+
+        def entries(lst, ms):
+            return lst[:, ms.start // 16 : ms.stop // 16]
+
         def donor(s):
-            b, i = divmod(s, 4)
-            h1 = ring.tile([P, S], F32, name="h1")
+            h1[s] = ring.tile([P, S], F32, name="h1", bufs=3)
             for h in range(2):
                 cols = slice(BANK * h, BANK * (h + 1))
                 first = product8(1, s, h)
                 second = product4(s, h)
-                d1 = ring.tile([P, BANK], F32, name="d1", bufs=4)
-                nc.scalar.activation(out=d1[:], in_=first[:], func=ACT.Identity, bias=bias1[:, s : s + 1])
-                nc.vector.tensor_tensor(out=h1[:, cols], in0=second[:], in1=d1[:], op=ALU.max)
-            nc.vector.tensor_tensor(out=xa[b][:, i, :], in0=h1[:].indirect(list2[:]), in1=ga, op=ALU.mult)
+                if h == 0 and s > 0:
+                    d1 = xa[(s - 1) // 4][:, (s - 1) % 4, :]
+                else:
+                    d1 = ring.tile([P, BANK], F32, name="d1", bufs=3)[:]
+                nc.scalar.activation(out=d1, in_=first[:], func=ACT.Identity, bias=bias1[:, s : s + 1])
+                nc.vector.tensor_tensor(out=h1[s][:, cols], in0=second[:], in1=d1, op=ALU.max)
+
+        def pick_donor(s, ms):
+            b, i = divmod(s, 4)
+            nc.vector.tensor_tensor(
+                out=xa[b][:, i, ms], in0=h1[s][:].indirect(entries(list2, ms)), in1=ga[:, ms], op=ALU.mult
+            )
 
         def recipient(s):
-            b, i = divmod(s, 4)
-            h2 = ring.tile([P, S], F32, name="h2", bufs=3)
+            h2[s] = ring.tile([P, S], F32, name="h2", bufs=5)
             for h in range(2):
                 third = product8(3, s, h)
                 nc.scalar.activation(
-                    out=h2[:, BANK * h : BANK * (h + 1)], in_=third[:], func=ACT.Identity, bias=bias3[:, s : s + 1]
+                    out=h2[s][:, BANK * h : BANK * (h + 1)], in_=third[:], func=ACT.Identity, bias=bias3[:, s : s + 1]
                 )
-            xb = ring.tile([P, M], F32, name="xb")
-            nc.vector.tensor_tensor(out=xb[:], in0=h2[:].indirect(list3[:]), in1=gb, op=ALU.mult)
-            nc.scalar.activation(out=th[b][:, i, :], in_=xb[:], func=ACT.Tanh)
 
-        def make_z(b):
-            zb = ring.tile([P, M, 4], BF16, name="zb", align_bytes=64)
+        def pick_recipient(s, ms):
+            b, i = divmod(s, 4)
+            xb = ring.tile([P, ms.stop - ms.start], F32, name="xb", bufs=4)
+            nc.vector.tensor_tensor(out=xb[:], in0=h2[s][:].indirect(entries(list3, ms)), in1=gb[:, ms], op=ALU.mult)
+            nc.scalar.activation(out=th[b][:, i, ms], in_=xb[:], func=ACT.Tanh)
+
+        def make_z(b, ms):
+            zb = ring.tile([P, ms.stop - ms.start, 4], BF16, name="zb", align_bytes=64)
             nc.vector.tensor_tensor(
                 out=zb[:].rearrange("p (c e) i -> p c i e", e=4),
-                in0=xa[b][:].rearrange("p i (c e) -> p c i e", e=4),
-                in1=th[b][:].rearrange("p i (c e) -> p c i e", e=4),
+                in0=xa[b][:, :, ms].rearrange("p i (c e) -> p c i e", e=4),
+                in1=th[b][:, :, ms].rearrange("p i (c e) -> p c i e", e=4),
                 op=ALU.mult,
             )
             return zb
 
-        def quant_z(b, zb):
-            nc.vector.quantize_mx(out=zc[b][:].bitcast(FP8X4), scales=zs[b][:], in_=zb[:].rearrange("p m i -> p (m i)"))
+        def quant_z(b, ms, zb):
+            nc.vector.quantize_mx(
+                out=zc[b][:, ms].bitcast(FP8X4), scales=zs[b][:, ms], in_=zb[:].rearrange("p m i -> p (m i)")
+            )
 
-        def last_pass(acc, s, a):
-            nc.tensor.matmul_mx(
-                out=acc[:],
-                lhsT=w4c[a][:, 2 * P * s : 2 * P * (s + 1)].bitcast(FP4X4),
-                lhsT_scale=w4s[:, a, P * s : P * (s + 1)],
-                rhs=zc[a][:].bitcast(FP8X4),
-                rhs_scale=zs[a][:],
-                start=(a == 0), stop=(a == 1),
+        def last_passes(accs, f, a):
+            ms = halves[f]
+            for s in range(8):
+                nc.tensor.matmul_mx(
+                    out=accs[s // 2][:, s % 2, :],
+                    lhsT=w4c[a][:, 2 * P * s : 2 * P * (s + 1)].bitcast(FP4X4),
+                    lhsT_scale=w4s[:, a, P * s : P * (s + 1)],
+                    rhs=zc[a][:, ms].bitcast(FP8X4),
+                    rhs_scale=zs[a][:, ms],
+                    start=(a == 0 and s % 2 == 0), stop=(a == 1 and s % 2 == 1),
+                )
+
+        def add_sed(accs, f, g):
+            ms = halves[f]
+            y = ring.tile([P, 4, M // 2], F32, name="y", bufs=4)
+            for u in range(2):
+                nc.vector.tensor_tensor(
+                    out=y[:, 2 * u : 2 * u + 2, :], in0=accs[2 * g + u][:], in1=sedt[g][:, 2 * u : 2 * u + 2, ms], op=ALU.add
+                )
+            nc.sync.dma_start(
+                out=out_0[BANK * g : BANK * (g + 1), ms].rearrange("(p t) m -> p t m", t=4), in_=y[:]
+            )
+            return y
+
+        def round_y(copy, y):
+            yb = ring.tile([P, M // 2, 4], BF16, name="yb", bufs=4, align_bytes=64)
+            copy(out=yb[:].rearrange("p (c e) t -> p c t e", e=4), in_=y[:].rearrange("p t (c e) -> p c t e", e=4))
+            return yb
+
+        def quant_y(f, g, yb):
+            ms = halves[f]
+            yc = ring.tile([P, M // 2], U32, name="yc", bufs=4, align_bytes=64)
+            nc.vector.quantize_mx(out=yc[:].bitcast(FP8X4), scales=ys[:, g, ms], in_=yb[:].rearrange("p m t -> p (m t)"))
+            nc.sync.dma_start(
+                out=out_1[g, :, ms, :].rearrange("p m t -> p (m t)").bitcast(I32), in_=yc[:].bitcast(I32)
             )
 
         donor(0)
         donor(1)
-        quant_w(3, 0, round_w(3, 0))
-        sedt = [load_sed(0, stage("sed0"))]
+        pick_donor(0, whole)
         donor(2)
-        recipient(0)
+        wb11 = round_w(1, 1)
+        sedt = [load_sed(0, stage("sed0"))]
+        pick_donor(1, whole)
+        quant_w(1, 1, wb11)
         donor(3)
         w4s = held.tile([P, 2, N], U8, name="w4s", tag="wc10", align_bytes=64)
         nc.gpsimd.memset(w4s[:].rearrange("p a c -> p (a c)").bitcast(I32), 0)
@@ -243,54 +291,64 @@ def tile_list_seagrass_clone_mixing_kernel(
                     out=w4s[32 * q : 32 * q + 4, a, :].bitcast(I32),
                     in_=dealt4[32 * q + 4 + 4 * a : 32 * q + 8 + 4 * a, :].bitcast(I32),
                 )
-        recipient(1)
-        quant_w(1, 1, round_w(1, 1))
-        recipient(2)
-        recipient(3)
+        pick_donor(2, whole)
         donor(4)
+        pick_donor(3, whole)
+        donor(5)
+        wb30 = round_w(3, 0)
+        pick_donor(4, whole)
+        quant_w(3, 0, wb30)
+        donor(6)
+        pick_donor(5, whole)
+        donor(7)
+        pick_donor(6, whole)
+        for s in range(4):
+            recipient(s)
         wb31 = round_w(3, 1)
         w4raw = held.tile([P, 2, 2 * N], U8, name="w4raw", tag="big", align_bytes=64)
         for a in range(2):
             nc.sync.dma_start(out=w4raw[:, a, :].bitcast(I32), in_=w4_words[a].bitcast(I32))
-        zb0 = make_z(0)
+        pick_recipient(0, whole)
+        pick_donor(7, whole)
         quant_w(3, 1, wb31)
-        sedt.append(load_sed(1, held.tile([P, 4, M], F32, name="sed1", tag="xa0", align_bytes=64)))
-        donor(5)
-        quant_z(0, zb0)
+        pick_recipient(1, whole)
+        pick_recipient(2, whole)
         recipient(4)
-        donor(6)
+        pick_recipient(3, whole)
         recipient(5)
+        zb0 = make_z(0, whole)
+        sedt.append(load_sed(1, held.tile([P, 4, M], F32, name="sed1", tag="xa0", align_bytes=64)))
         recipient(6)
         recipient(7)
-        donor(7)
+        pick_recipient(4, halves[0])
+        quant_z(0, whole, zb0)
+        for s in range(5, 8):
+            pick_recipient(s, halves[0])
         for a in range(2):
             deal_words(nc.scalar.copy, w4c[a][:], w4raw[:, a, :])
-        accs = [psum.tile([P, BANK], F32, name="acc") for s in range(8)]
-        for s in range(8):
-            last_pass(accs[s], s, 0)
-        quant_z(1, make_z(1))
-        for s in range(8):
-            last_pass(accs[s], s, 1)
+        accs = [[psum.tile([P, 2, M // 2], F32, name="acc") for u in range(4)] for f in range(2)]
+        for f in range(2):
+            last_passes(accs[f], f, 0)
+        pick_recipient(4, halves[1])
+        zb = make_z(1, halves[0])
+        pick_recipient(5, halves[1])
+        quant_z(1, halves[0], zb)
+        last_passes(accs[0], 0, 1)
+        pick_recipient(6, halves[1])
+        pick_recipient(7, halves[1])
+        y = [add_sed(accs[0], 0, g) for g in range(2)]
+        yb = [round_y(nc.scalar.copy, y[g]) for g in range(2)]
+        zb = make_z(1, halves[1])
+        quant_y(0, 0, yb[0])
+        quant_z(1, halves[1], zb)
+        last_passes(accs[1], 1, 1)
+        quant_y(0, 1, yb[1])
+        y = [add_sed(accs[1], 1, g) for g in range(2)]
+        yb = [round_y(nc.scalar.copy, y[0]), round_y(nc.vector.tensor_copy, y[1])]
         for g in range(2):
-            for t in range(4):
-                nc.vector.tensor_tensor(out=y[g][:, t, :], in0=accs[4 * g + t][:], in1=sedt[g][:, t, :], op=ALU.add)
-            nc.sync.dma_start(
-                out=out_0[BANK * g : BANK * (g + 1), :].rearrange("(p t) m -> p t m", t=4), in_=y[g][:]
+            quant_y(1, g, yb[g])
+        for q in range(4):
+            nc.scalar.dma_start(
+                out=out_2[:, 4 * q : 4 * q + 4, :].rearrange("g r m -> r g m").bitcast(I32),
+                in_=ys[32 * q : 32 * q + 4, :, :].bitcast(I32),
             )
-        for g in range(2):
-            yb = ring.tile([P, M, 4], BF16, name="yb", align_bytes=64)
-            src = y[g][:].rearrange("p t (c e) -> p c t e", e=4)
-            dst = yb[:].rearrange("p (c e) t -> p c t e", e=4)
-            if g == 0:
-                nc.scalar.copy(out=dst, in_=src)
-            else:
-                nc.vector.tensor_copy(out=dst, in_=src)
-            nc.vector.quantize_mx(out=yc[g][:].bitcast(FP8X4), scales=ys[g][:], in_=yb[:].rearrange("p m t -> p (m t)"))
-            nc.sync.dma_start(
-                out=out_1[g].rearrange("p m t -> p (m t)").bitcast(I32), in_=yc[g][:].bitcast(I32)
-            )
-            for q in range(4):
-                nc.scalar.dma_start(
-                    out=out_2[g, 4 * q : 4 * q + 4, :].bitcast(I32),
-                    in_=ys[g][32 * q : 32 * q + 4, :].bitcast(I32),
-                )

from contextlib import ExitStack

import concourse.mybir as mybir

K, H, N, T, S, M = 512, 1024, 1024, 4096, 1024, 512
FLOPS = 2 * (3 * K * H * S + H * N * M)

F32 = mybir.dt.float32
BF16 = mybir.dt.bfloat16
I32 = mybir.dt.int32
U32 = mybir.dt.uint32
U16 = mybir.dt.uint16
U8 = mybir.dt.uint8
FP8X4 = mybir.dt.float8_e4m3fn_x4
FP4X4 = mybir.dt.float4_e2m1fn_x4
ACT = mybir.ActivationFunctionType
ALU = mybir.AluOpType
P = 128
BANK = 512


def tile_list_seagrass_clone_mixing_kernel(
    tc, tab_words, tab_scales, offs, w1, b1, w2_words, w2_scales, w3, b3, offs2, offs3,
    wga, wgb, w4_words, w4_scales, sed, out_0, out_1, out_2,
):
    nc = tc.nc
    with ExitStack() as ctx:
        held = ctx.enter_context(tc.tile_pool(name="held", bufs=1))
        ring = ctx.enter_context(tc.tile_pool(name="ring", bufs=2))
        psum = ctx.enter_context(tc.psum_pool(name="psum", bufs=8))

        def keep(name, shape, dtype):
            return held.tile(shape, dtype, name=name, align_bytes=64)

        list1 = held.tile([P, S // 16], U16, name="list1")
        list2 = held.tile([P, M // 16], U16, name="list2")
        list3 = held.tile([P, M // 16], U16, name="list3")
        tabs = held.tile([P, T], U8, name="tabs", tag="bytes", align_bytes=64)
        packed = held.tile([P, H], U8, name="packed", tag="packed", align_bytes=64)
        packed4 = keep("packed4", [P, N], U8)
        dealt4 = keep("dealt4", [P, N], U8)
        w2raw = held.tile([P, 2 * H], U8, name="w2raw", tag="big", align_bytes=64)
        w2c = keep("w2c", [P, 2 * H], U8)
        w4c = [keep(f"w4c{a}", [P, 2 * N], U8) for a in range(2)]
        wraw = {}
        wc = {(n, b): held.tile([P, BANK], U32, name=f"wc{n}{b}", tag=f"wc{n}{b}", align_bytes=64) for n in (1, 3) for b in range(2)}
        ws = {(n, b): keep(f"ws{n}{b}", [P, BANK], U8) for n in (1, 3) for b in range(2)}
        bias1 = keep("bias1", [P, 8], F32)
        bias3 = keep("bias3", [P, 8], F32)
        vc = [keep(f"vc{h}", [P, BANK], U32) for h in range(2)]
        vs = keep("vs", [P, S], U8)
        picked = keep("picked", [P, S], U8)
        zc = [keep(f"zc{b}", [P, M], U32) for b in range(2)]
        zs = [keep(f"zs{b}", [P, M], U8) for b in range(2)]
        ys = keep("ys", [P, 2, M], U8)
        xa = [held.tile([P, 4, M], F32, name=f"xa{b}", tag=f"xa{b}", align_bytes=64) for b in range(2)]
        th = [keep(f"th{b}", [P, 4, M], F32) for b in range(2)]

        def load_w(n, src, b, dst):
            wraw[n, b] = dst
            nc.sync.dma_start(out=dst, in_=src[:, BANK * b : BANK * (b + 1)].rearrange("(p j) c -> p j c", j=4))

        def stage(name):
            return held.tile([P, 4, BANK], F32, name=name, tag="stage", align_bytes=64)

        nc.vector.memset(tabs[:].bitcast(I32), 0)
        nc.gpsimd.memset(packed[:].bitcast(I32), 0)
        for q in range(4):
            nc.gpsimd.dma_start(
                out=packed[32 * q : 32 * q + 4, :].bitcast(I32),
                in_=w2_scales[0, 4 * q : 4 * q + 4, :].bitcast(I32),
            )
        nc.gpsimd.memset(vs[:].bitcast(I32), 0)
        nc.gpsimd.memset(packed4[:].bitcast(I32), 0)
        for q in range(4):
            nc.gpsimd.dma_start(
                out=packed4[32 * q + 4 : 32 * q + 12, :].bitcast(I32),
                in_=w4_scales[:, 4 * q : 4 * q + 4, :].bitcast(I32),
            )
        nc.gpsimd.tensor_copy(
            out=dealt4[:].rearrange("p (b i q) -> p b i q", b=2, i=4),
            in_=packed4[:].rearrange("p (b q i) -> p b i q", b=2, i=4),
        )

        nc.sync.dma_start(out=w2raw[:].bitcast(I32), in_=w2_words[0].bitcast(I32))
        nc.sync.dma_start(out=list1[:], in_=offs)
        nc.sync.dma_start(
            out=bias1[:].rearrange("p (b i) -> p b i", b=2),
            in_=b1.rearrange("(b p i) -> p b i", b=2, i=4),
        )
        nc.sync.dma_start(out=list2[:], in_=offs2)
        load_w(1, w1, 0, stage("w10")[:])
        nc.sync.dma_start(out=list3[:], in_=offs3)
        nc.sync.dma_start(
            out=bias3[:].rearrange("p (b i) -> p b i", b=2),
            in_=b3.rearrange("(b p i) -> p b i", b=2, i=4),
        )
        nc.scalar.dma_start(out=tabs[0:P:8, :].bitcast(I32), in_=tab_scales[0].bitcast(I32))

        def load_sed(g, dst):
            nc.sync.dma_start(
                out=dst[:], in_=sed[BANK * g : BANK * (g + 1), :].rearrange("(p t) m -> p t m", t=4)
            )
            return dst

        def round_w(n, b):
            if (n, b) == (1, 0):
                wb = held.tile([P, 4, P, 4], BF16, name="wb_first", tag="first", align_bytes=64)
            else:
                wb = ring.tile([P, 4, P, 4], BF16, name="wb", align_bytes=64)
            nc.scalar.copy(
                out=wb[:].rearrange("p i q j -> p q j i"),
                in_=wraw[n, b].rearrange("p j (q i) -> p q j i", i=4),
            )
            return wb

        def quant_w(n, b, wb):
            nc.vector.quantize_mx(
                out=wc[n, b][:].bitcast(FP8X4),
                scales=ws[n, b][:],
                in_=wb[:].rearrange("p i q j -> p (i q j)"),
            )

        def deal_words(copy, dst, src):
            copy(
                out=dst.bitcast(U16).rearrange("p (b i c q) -> p b c i q", b=2, i=4, q=8),
                in_=src.bitcast(U16).rearrange("p (b c q i) -> p b c i q", b=2, i=4, q=8),
            )

        deal_words(nc.vector.tensor_copy, w2c[:], w2raw[:])
        tabw = held.tile([P, T], U32, name="tabw", tag="big", align_bytes=64)
        nc.sync.dma_start(
            out=tabw[:].bitcast(I32),
            in_=tab_words[0].rearrange("p t i -> p (t i)").bitcast(I32),
        )
        wb10 = round_w(1, 0)
        nc.vector.tensor_copy(out=picked[:], in_=tabs[:].indirect(list1[:]))
        for q in range(4):
            nc.sync.dma_start(
                out=vs[32 * q : 32 * q + 4, :].bitcast(I32),
                in_=picked[32 * q : 32 * q + 32 : 8, :].bitcast(I32),
            )
        load_w(1, w1, 1, stage("w11")[:])
        quant_w(1, 0, wb10)
        dealt = held.tile([P, H], U8, name="dealt", tag="first", align_bytes=64)
        nc.vector.tensor_copy(
            out=dealt[:].rearrange("p (b i q) -> p b i q", b=2, i=4),
            in_=packed[:].rearrange("p (b q i) -> p b i q", b=2, i=4),
        )
        gab = held.tile([P, 2, M], F32, name="gab", tag="packed", align_bytes=64)
        ga, gb = gab[:, 0, :], gab[:, 1, :]
        nc.sync.dma_start(out=ga, in_=wga)
        nc.sync.dma_start(out=gb, in_=wgb)
        for h in range(2):
            nc.vector.tensor_copy(out=vc[h][:], in_=tabw[:].indirect(list1[:, 32 * h : 32 * (h + 1)]))
        late = held.tile([P, 2, 4, BANK], F32, name="late", tag="big", align_bytes=64)
        load_w(3, w3, 0, late[:, 0])
        load_w(3, w3, 1, late[:, 1])

        def product8(n, s, h):
            b, i = divmod(s, 4)
            acc = psum.tile([P, BANK], F32, name="acc")
            nc.tensor.matmul_mx(
                out=acc[:],
                lhsT=wc[n, b][:, P * i : P * (i + 1)].bitcast(FP8X4),
                lhsT_scale=ws[n, b][:, P * i : P * (i + 1)],
                rhs=vc[h][:].bitcast(FP8X4),
                rhs_scale=vs[:, BANK * h : BANK * (h + 1)],
                start=True, stop=True,
            )
            return acc

        def product4(s, h):
            acc = psum.tile([P, BANK], F32, name="acc")
            nc.tensor.matmul_mx(
                out=acc[:],
                lhsT=w2c[:, 2 * P * s : 2 * P * (s + 1)].bitcast(FP4X4),
                lhsT_scale=dealt[:, P * s : P * (s + 1)],
                rhs=vc[h][:].bitcast(FP8X4),
                rhs_scale=vs[:, BANK * h : BANK * (h + 1)],
                start=True, stop=True,
            )
            return acc

        h1, h2 = {}, {}
        whole = slice(0, M)
        halves = [slice(0, M // 2), slice(M // 2, M)]

        def entries(lst, ms):
            return lst[:, ms.start // 16 : ms.stop // 16]

        def donor(s):
            h1[s] = ring.tile([P, S], F32, name="h1", bufs=3)
            for h in range(2):
                cols = slice(BANK * h, BANK * (h + 1))
                first = product8(1, s, h)
                second = product4(s, h)
                if h == 0 and s > 0:
                    d1 = xa[(s - 1) // 4][:, (s - 1) % 4, :]
                else:
                    d1 = ring.tile([P, BANK], F32, name="d1", bufs=3)[:]
                nc.scalar.activation(out=d1, in_=first[:], func=ACT.Identity, bias=bias1[:, s : s + 1])
                nc.vector.tensor_tensor(out=h1[s][:, cols], in0=second[:], in1=d1, op=ALU.max)

        def pick_donor(s, ms):
            b, i = divmod(s, 4)
            nc.vector.tensor_tensor(
                out=xa[b][:, i, ms], in0=h1[s][:].indirect(entries(list2, ms)), in1=ga[:, ms], op=ALU.mult
            )

        def recipient(s):
            h2[s] = ring.tile([P, S], F32, name="h2", bufs=5)
            for h in range(2):
                third = product8(3, s, h)
                nc.scalar.activation(
                    out=h2[s][:, BANK * h : BANK * (h + 1)], in_=third[:], func=ACT.Identity, bias=bias3[:, s : s + 1]
                )

        def pick_recipient(s, ms):
            b, i = divmod(s, 4)
            xb = ring.tile([P, ms.stop - ms.start], F32, name="xb", bufs=4)
            nc.vector.tensor_tensor(out=xb[:], in0=h2[s][:].indirect(entries(list3, ms)), in1=gb[:, ms], op=ALU.mult)
            nc.scalar.activation(out=th[b][:, i, ms], in_=xb[:], func=ACT.Tanh)

        def make_z(b, ms):
            zb = ring.tile([P, ms.stop - ms.start, 4], BF16, name="zb", align_bytes=64)
            nc.vector.tensor_tensor(
                out=zb[:].rearrange("p (c e) i -> p c i e", e=4),
                in0=xa[b][:, :, ms].rearrange("p i (c e) -> p c i e", e=4),
                in1=th[b][:, :, ms].rearrange("p i (c e) -> p c i e", e=4),
                op=ALU.mult,
            )
            return zb

        def quant_z(b, ms, zb):
            nc.vector.quantize_mx(
                out=zc[b][:, ms].bitcast(FP8X4), scales=zs[b][:, ms], in_=zb[:].rearrange("p m i -> p (m i)")
            )

        def last_passes(accs, f, a):
            ms = halves[f]
            for s in range(8):
                nc.tensor.matmul_mx(
                    out=accs[s // 2][:, s % 2, :],
                    lhsT=w4c[a][:, 2 * P * s : 2 * P * (s + 1)].bitcast(FP4X4),
                    lhsT_scale=w4s[:, a, P * s : P * (s + 1)],
                    rhs=zc[a][:, ms].bitcast(FP8X4),
                    rhs_scale=zs[a][:, ms],
                    start=(a == 0 and s % 2 == 0), stop=(a == 1 and s % 2 == 1),
                )

        def add_sed(accs, f, g):
            ms = halves[f]
            y = ring.tile([P, 4, M // 2], F32, name="y", bufs=4)
            for u in range(2):
                nc.vector.tensor_tensor(
                    out=y[:, 2 * u : 2 * u + 2, :], in0=accs[2 * g + u][:], in1=sedt[g][:, 2 * u : 2 * u + 2, ms], op=ALU.add
                )
            nc.sync.dma_start(
                out=out_0[BANK * g : BANK * (g + 1), ms].rearrange("(p t) m -> p t m", t=4), in_=y[:]
            )
            return y

        def round_y(copy, y):
            yb = ring.tile([P, M // 2, 4], BF16, name="yb", bufs=4, align_bytes=64)
            copy(out=yb[:].rearrange("p (c e) t -> p c t e", e=4), in_=y[:].rearrange("p t (c e) -> p c t e", e=4))
            return yb

        def quant_y(f, g, yb):
            ms = halves[f]
            yc = ring.tile([P, M // 2], U32, name="yc", bufs=4, align_bytes=64)
            nc.vector.quantize_mx(out=yc[:].bitcast(FP8X4), scales=ys[:, g, ms], in_=yb[:].rearrange("p m t -> p (m t)"))
            nc.sync.dma_start(
                out=out_1[g, :, ms, :].rearrange("p m t -> p (m t)").bitcast(I32), in_=yc[:].bitcast(I32)
            )

        donor(0)
        donor(1)
        pick_donor(0, whole)
        donor(2)
        wb11 = round_w(1, 1)
        sedt = [load_sed(0, stage("sed0"))]
        pick_donor(1, whole)
        quant_w(1, 1, wb11)
        donor(3)
        w4s = held.tile([P, 2, N], U8, name="w4s", tag="wc10", align_bytes=64)
        nc.gpsimd.memset(w4s[:].rearrange("p a c -> p (a c)").bitcast(I32), 0)
        for a in range(2):
            for q in range(4):
                nc.sync.dma_start(
                    out=w4s[32 * q : 32 * q + 4, a, :].bitcast(I32),
                    in_=dealt4[32 * q + 4 + 4 * a : 32 * q + 8 + 4 * a, :].bitcast(I32),
                )
        pick_donor(2, whole)
        donor(4)
        pick_donor(3, whole)
        donor(5)
        wb30 = round_w(3, 0)
        pick_donor(4, whole)
        quant_w(3, 0, wb30)
        donor(6)
        pick_donor(5, whole)
        donor(7)
        pick_donor(6, whole)
        for s in range(4):
            recipient(s)
        wb31 = round_w(3, 1)
        w4raw = held.tile([P, 2, 2 * N], U8, name="w4raw", tag="big", align_bytes=64)
        for a in range(2):
            nc.sync.dma_start(out=w4raw[:, a, :].bitcast(I32), in_=w4_words[a].bitcast(I32))
        pick_recipient(0, whole)
        pick_donor(7, whole)
        quant_w(3, 1, wb31)
        pick_recipient(1, whole)
        pick_recipient(2, whole)
        recipient(4)
        pick_recipient(3, whole)
        recipient(5)
        zb0 = make_z(0, whole)
        sedt.append(load_sed(1, held.tile([P, 4, M], F32, name="sed1", tag="xa0", align_bytes=64)))
        recipient(6)
        recipient(7)
        pick_recipient(4, halves[0])
        quant_z(0, whole, zb0)
        for s in range(5, 8):
            pick_recipient(s, halves[0])
        for a in range(2):
            deal_words(nc.scalar.copy, w4c[a][:], w4raw[:, a, :])
        accs = [[psum.tile([P, 2, M // 2], F32, name="acc") for u in range(4)] for f in range(2)]
        for f in range(2):
            last_passes(accs[f], f, 0)
        pick_recipient(4, halves[1])
        zb = make_z(1, halves[0])
        pick_recipient(5, halves[1])
        quant_z(1, halves[0], zb)
        last_passes(accs[0], 0, 1)
        pick_recipient(6, halves[1])
        pick_recipient(7, halves[1])
        y = [add_sed(accs[0], 0, g) for g in range(2)]
        yb = [round_y(nc.scalar.copy, y[g]) for g in range(2)]
        zb = make_z(1, halves[1])
        quant_y(0, 0, yb[0])
        quant_z(1, halves[1], zb)
        last_passes(accs[1], 1, 1)
        quant_y(0, 1, yb[1])
        y = [add_sed(accs[1], 1, g) for g in range(2)]
        yb = [round_y(nc.scalar.copy, y[0]), round_y(nc.vector.tensor_copy, y[1])]
        for g in range(2):
            quant_y(1, g, yb[g])
        for q in range(4):
            nc.scalar.dma_start(
                out=out_2[:, 4 * q : 4 * q + 4, :].rearrange("g r m -> r g m").bitcast(I32),
                in_=ys[32 * q : 32 * q + 4, :, :].bitcast(I32),
            )
